import numpy as np
import ml_dtypes

BF16 = ml_dtypes.bfloat16


def bf(x):
    return np.asarray(x, np.float32).astype(BF16)


def f32(x):
    return np.asarray(x, np.float32)


def f64(x):
    return np.asarray(x).astype(np.float64)


def striped(idx):
    return np.tile(idx.reshape(-1, 16).T, (8, 1))


S, K, M, N, V, F = 1024, 128, 128, 4096, 512, 8


def setup_inputs():
    return {"table": bf(np.random.standard_normal((F, K, S))), "w": bf(np.random.standard_normal((F, K, M)) / np.sqrt(F * K)), "offs": striped(np.concatenate([np.random.permutation(np.tile(np.arange(S), 2))[:V] for _ in range(F)]))}


def reference(table, w, offs):
    idx = offs[:16].T.reshape(-1)
    y = sum(f64(w)[f].T @ f64(table)[f][:, idx[f * V : (f + 1) * V]] for f in range(F))
    return y

@@ -1,0 +1,33 @@
+import concourse.mybir as mybir
+
+BF16, F32, U16 = mybir.dt.bfloat16, mybir.dt.float32, mybir.dt.uint16
+
+FIELDS, FEATURES, VALUES = 8, 128, 1024
+OUTPUTS, SAMPLES = 128, 512
+ENTRIES_PER_COLUMN = 16
+
+FLOPS = 2 * FIELDS * FEATURES * OUTPUTS * SAMPLES
+
+
+def tile_rows_fields_none_rep_kernel(tc, table, w, offs, out):
+    nc = tc.nc
+    field_columns = SAMPLES // ENTRIES_PER_COLUMN
+    with (
+        tc.tile_pool(name="held", bufs=1) as held,
+        tc.psum_pool(name="psum", bufs=1) as psum,
+    ):
+        offsets = held.tile([128, FIELDS * field_columns], U16, name="offsets")
+        nc.sync.dma_start(offsets[:], offs)
+        weights = held.tile([FEATURES, FIELDS, OUTPUTS], BF16, name="weights")
+        nc.scalar.dma_start(weights[:], w.rearrange("f k m -> k f m"))
+
+        sums = psum.tile([OUTPUTS, SAMPLES], F32, name="sums")
+        for f in range(FIELDS):
+            window = held.tile([FEATURES, VALUES], BF16, name=f"window{f}")
+            nc.sync.dma_start(window[:], table[f])
+            picked = window[:].indirect(offsets[:, f * field_columns : (f + 1) * field_columns])
+            nc.tensor.matmul(sums[:], weights[:, f, :], picked, start=(f == 0), stop=(f == FIELDS - 1))
+
+        result = held.tile([OUTPUTS, SAMPLES], F32, name="result")
+        nc.vector.tensor_copy(result[:], sums[:])
+        nc.sync.dma_start(out, result[:])

@@ -8,26 +8,51 @@ ENTRIES_PER_COLUMN = 16
 
 FLOPS = 2 * FIELDS * FEATURES * OUTPUTS * SAMPLES
 
+HALVES = 2
+HALF = SAMPLES // HALVES
+LATE_FIELDS = 2
+EARLY_FIELDS = FIELDS - LATE_FIELDS
+
 
 def tile_rows_fields_none_rep_kernel(tc, table, w, offs, out):
     nc = tc.nc
-    field_columns = SAMPLES // ENTRIES_PER_COLUMN
     with (
         tc.tile_pool(name="held", bufs=1) as held,
         tc.psum_pool(name="psum", bufs=1) as psum,
     ):
-        offsets = held.tile([128, FIELDS * field_columns], U16, name="offsets")
+        offsets = held.tile([128, FIELDS * SAMPLES // ENTRIES_PER_COLUMN], U16, name="offsets")
         nc.sync.dma_start(offsets[:], offs)
         weights = held.tile([FEATURES, FIELDS, OUTPUTS], BF16, name="weights")
         nc.scalar.dma_start(weights[:], w.rearrange("f k m -> k f m"))
-
-        sums = psum.tile([OUTPUTS, SAMPLES], F32, name="sums")
+        windows = [held.tile([FEATURES, VALUES], BF16, name=f"window{f}") for f in range(FIELDS)]
         for f in range(FIELDS):
-            window = held.tile([FEATURES, VALUES], BF16, name=f"window{f}")
-            nc.sync.dma_start(window[:], table[f])
-            picked = window[:].indirect(offsets[:, f * field_columns : (f + 1) * field_columns])
-            nc.tensor.matmul(sums[:], weights[:, f, :], picked, start=(f == 0), stop=(f == FIELDS - 1))
+            nc.sync.dma_start(windows[f][:], table[f])
 
-        result = held.tile([OUTPUTS, SAMPLES], F32, name="result")
-        nc.vector.tensor_copy(result[:], sums[:])
-        nc.sync.dma_start(out, result[:])
+        def picked(f, first_sample, count):
+            column = (f * SAMPLES + first_sample) // ENTRIES_PER_COLUMN
+            return windows[f][:].indirect(offsets[:, column : column + count // ENTRIES_PER_COLUMN])
+
+        early_sums = psum.tile([OUTPUTS, SAMPLES], F32, name="early_sums")
+        for f in range(EARLY_FIELDS):
+            nc.tensor.matmul(
+                early_sums[:], weights[:, f, :], picked(f, 0, SAMPLES), start=(f == 0), stop=(f == EARLY_FIELDS - 1)
+            )
+        early = held.tile([OUTPUTS, SAMPLES], F32, name="early")
+        nc.vector.tensor_copy(early[:], early_sums[:])
+
+        late_sums = [psum.tile([OUTPUTS, HALF], F32, name=f"late_sums{h}") for h in range(HALVES)]
+        for f in range(EARLY_FIELDS, FIELDS):
+            for h in range(HALVES):
+                nc.tensor.matmul(
+                    late_sums[h][:],
+                    weights[:, f, :],
+                    picked(f, h * HALF, HALF),
+                    start=(f == EARLY_FIELDS),
+                    stop=(f == FIELDS - 1),
+                )
+
+        for h, queue in enumerate((nc.sync, nc.scalar)):
+            samples = slice(h * HALF, (h + 1) * HALF)
+            result = held.tile([OUTPUTS, HALF], F32, name=f"result{h}")
+            nc.vector.tensor_tensor(result[:], late_sums[h][:], early[:, samples], mybir.AluOpType.add)
+            queue.dma_start(out[:, samples], result[:])

import concourse.mybir as mybir

BF16, F32, U16 = mybir.dt.bfloat16, mybir.dt.float32, mybir.dt.uint16

FIELDS, FEATURES, VALUES = 8, 128, 1024
OUTPUTS, SAMPLES = 128, 512
ENTRIES_PER_COLUMN = 16

FLOPS = 2 * FIELDS * FEATURES * OUTPUTS * SAMPLES

HALVES = 2
HALF = SAMPLES // HALVES
LATE_FIELDS = 2
EARLY_FIELDS = FIELDS - LATE_FIELDS


def tile_rows_fields_none_rep_kernel(tc, table, w, offs, out):
    nc = tc.nc
    with (
        tc.tile_pool(name="held", bufs=1) as held,
        tc.psum_pool(name="psum", bufs=1) as psum,
    ):
        offsets = held.tile([128, FIELDS * SAMPLES // ENTRIES_PER_COLUMN], U16, name="offsets")
        nc.sync.dma_start(offsets[:], offs)
        weights = held.tile([FEATURES, FIELDS, OUTPUTS], BF16, name="weights")
        nc.scalar.dma_start(weights[:], w.rearrange("f k m -> k f m"))
        windows = [held.tile([FEATURES, VALUES], BF16, name=f"window{f}") for f in range(FIELDS)]
        for f in range(FIELDS):
            nc.sync.dma_start(windows[f][:], table[f])

        def picked(f, first_sample, count):
            column = (f * SAMPLES + first_sample) // ENTRIES_PER_COLUMN
            return windows[f][:].indirect(offsets[:, column : column + count // ENTRIES_PER_COLUMN])

        early_sums = psum.tile([OUTPUTS, SAMPLES], F32, name="early_sums")
        for f in range(EARLY_FIELDS):
            nc.tensor.matmul(
                early_sums[:], weights[:, f, :], picked(f, 0, SAMPLES), start=(f == 0), stop=(f == EARLY_FIELDS - 1)
            )
        early = held.tile([OUTPUTS, SAMPLES], F32, name="early")
        nc.vector.tensor_copy(early[:], early_sums[:])

        late_sums = [psum.tile([OUTPUTS, HALF], F32, name=f"late_sums{h}") for h in range(HALVES)]
        for f in range(EARLY_FIELDS, FIELDS):
            for h in range(HALVES):
                nc.tensor.matmul(
                    late_sums[h][:],
                    weights[:, f, :],
                    picked(f, h * HALF, HALF),
                    start=(f == EARLY_FIELDS),
                    stop=(f == FIELDS - 1),
                )

        for h, queue in enumerate((nc.sync, nc.scalar)):
            samples = slice(h * HALF, (h + 1) * HALF)
            result = held.tile([OUTPUTS, HALF], F32, name=f"result{h}")
            nc.vector.tensor_tensor(result[:], late_sums[h][:], early[:, samples], mybir.AluOpType.add)
            queue.dma_start(out[:, samples], result[:])
